import numpy as np
import ml_dtypes


def mxq(x, axis, fmt="e4m3"):
    dtype, down = {"e4m3": (ml_dtypes.float8_e4m3fn, 7), "e5m2": (ml_dtypes.float8_e5m2, 14)}[fmt]
    v = np.moveaxis(np.asarray(x, np.float32).astype(ml_dtypes.bfloat16).astype(np.float64), axis, -1)
    blocks = v.reshape(v.shape[:-1] + (-1, 32))
    amax = np.abs(blocks).max(-1, keepdims=True)
    byte = np.maximum(np.where(amax > 0, np.frexp(amax)[1] - 1 + 127, 0) - down, 1)
    scale = np.exp2(byte - 127.0)
    codes = (blocks / scale).astype(np.float32).astype(dtype).astype(np.float64)
    return np.moveaxis((codes * scale).reshape(v.shape), -1, axis)


WIDE = False


def mx_kscale(k):
    if not WIDE:
        return np.ones(k)
    levels = np.array([30, -30])
    if k % 512:
        return np.exp2(np.random.permutation(np.resize(levels, k // 32))).repeat(32)
    a = np.empty((k // 512, 16))
    for p in range(k // 512):
        a[p, :8] = np.random.permutation(np.resize(levels, 8))
        for g in range(8):
            far = levels[np.abs(levels - a[p, g]) >= 10]
            a[p, g + 8] = far[np.random.randint(len(far))]
    return np.exp2(a.ravel()).repeat(32)


def f64(x):
    return np.asarray(x).astype(np.float64)


def striped(idx):
    return np.tile(np.asarray(idx).reshape(-1, 16).T, (8, 1)).astype(np.uint16)


def unstriped(offs):
    return offs[:16].T.reshape(-1).astype(np.int64)


E2M1 = np.array([0.0, 0.5, 1.0, 1.5, 2.0, 3.0, 4.0, 6.0, -0.0, -0.5, -1.0, -1.5, -2.0, -3.0, -4.0, -6.0])


def pack_weight(w, fmt):
    k, n = w.shape
    w = f64(np.asarray(w, np.float32).astype(ml_dtypes.bfloat16)).reshape(k // 32, 32, n)
    amax = np.abs(w).max(1)
    if fmt == "e4m3":
        byte = np.frexp(amax)[1] - 1 + 127 - 7
    else:
        mant, ex = np.frexp(amax / 6.0)
        byte = np.where(mant > 0.5, ex, ex - 1) + 127
    byte = np.clip(np.where(amax > 0, byte, 1), 1, 254)
    scaled = (w * np.exp2(127.0 - byte)[:, None, :]).reshape(k, n).astype(np.float32)
    by_word = np.ascontiguousarray(scaled.reshape(k // 512, 128, 4, n).transpose(0, 1, 3, 2))
    if fmt == "e4m3":
        words = by_word.astype(ml_dtypes.float8_e4m3fn).view(np.uint8)
    else:
        c = by_word.astype(ml_dtypes.float4_e2m1fn).view(np.uint8) & 0xF
        words = (c[..., 0::2] | (c[..., 1::2] << 4)).reshape(k // 512, 128, 2 * n)
    return np.ascontiguousarray(words), np.ascontiguousarray(byte.astype(np.uint8).reshape(k // 512, 16, n))


def unpack_weight(words, scales, fmt):
    g, _, n = scales.shape
    words = np.ascontiguousarray(words).reshape(g, 128, n, -1)
    if fmt == "e4m3":
        vals = words.view(ml_dtypes.float8_e4m3fn).astype(np.float64)
    else:
        nib = np.empty((g, 128, n, 4), np.uint8)
        nib[..., 0::2] = words & 0xF
        nib[..., 1::2] = words >> 4
        vals = E2M1[nib]
    vals = vals * np.repeat(np.exp2(scales.astype(np.float64) - 127.0), 8, axis=1)[..., None]
    return vals.transpose(0, 1, 3, 2).reshape(g * 512, n)


K, T, J, N, C = 1024, 1024, 256, 256, 1024


def setup_inputs():
    n = np.random.standard_normal
    idx = np.random.permutation(T)[:J]
    idx2 = np.random.permutation(C)[:N]
    fk = mx_kscale(K)
    xtp = pack_weight(n((K, T)) * np.random.uniform(0.4, 1.6, (1, T)) / fk[:, None], "e2m1")
    wap = pack_weight(n((K, N)) * 1 / np.sqrt(K) * fk[:, None], "e2m1")
    return {
        "xt_words": xtp[0],
        "xt_scales": xtp[1],
        "wa_words": wap[0],
        "wa_scales": wap[1],
        "wb": (n((K, N)) * 1 / np.sqrt(K) * fk[:, None]).astype(np.float32),
        "bi": (np.random.uniform(-0.6, 0.6, (1, N))).astype(np.float32),
        "old": (1.0 * n((J, C))).astype(np.float32),
        "offs": striped(idx),
        "offs2": striped(idx2),
    }


def reference(xt_words, xt_scales, wa_words, wa_scales, wb, bi, old, offs, offs2):
    idx = unstriped(offs)
    idx2 = unstriped(offs2)
    xtu = unpack_weight(xt_words, xt_scales, "e2m1")
    wau = unpack_weight(wa_words, wa_scales, "e2m1")
    xtidxg = xtu[:, idx]
    a = xtidxg.T @ wau
    wbq = mxq(f64(wb), 0, "e5m2")
    b0 = xtidxg.T @ wbq
    b2 = b0 + f64(bi)
    d = np.maximum(a, b2)
    pp = np.zeros((J, C))
    pp[:, idx2] = d
    y = pp - 0.4 * f64(old)
    return y

@@ -1,0 +1,161 @@
+from contextlib import ExitStack
+
+import concourse.mybir as mybir
+from concourse.masks import make_identity
+
+K, T, J, N, C = 1024, 1024, 256, 256, 1024
+FLOPS = 2 * 2 * K * J * N
+
+F32 = mybir.dt.float32
+BF16 = mybir.dt.bfloat16
+I32 = mybir.dt.int32
+U32 = mybir.dt.uint32
+U16 = mybir.dt.uint16
+U8 = mybir.dt.uint8
+FP4X4 = mybir.dt.float4_e2m1fn_x4
+E5M2X4 = mybir.dt.float8_e5m2_x4
+ALU = mybir.AluOpType
+COPY = mybir.ActivationFunctionType.Copy
+
+P = 128
+PACK = 4
+K_PASS = P * PACK
+PASSES = K // K_PASS
+TILES = J // P
+LIST_COLS = P // 16
+V_COLS = (64, 160)
+OUT_COLS = 512
+
+
+def interleave_views(grouped, raw, c0, c1):
+    dst = grouped[:, c0:c1, :].rearrange("p (c i) t -> p c t i", i=4)
+    src = raw[:, :, c0:c1].rearrange("p t (c i) -> p c t i", i=4)
+    return dst, src
+
+
+def load_scale_rows(nc, plane, scales):
+    for q in range(4):
+        nc.sync.dma_start(
+            plane[32 * q : 32 * q + 4, :].bitcast(I32).rearrange("r (z c) -> r z c", z=PASSES),
+            scales[:, 4 * q : 4 * q + 4, :].bitcast(I32).rearrange("z r c -> r z c"),
+        )
+
+
+def tile_list_rows_onetoken_placedrows_kernel(
+    tc, xt_words, xt_scales, wa_words, wa_scales, wb, bi, old, offs, offs2, out
+):
+    nc = tc.nc
+    with ExitStack() as ctx:
+        sb = ctx.enter_context(tc.tile_pool(name="sb", bufs=1))
+        ps = ctx.enter_context(tc.psum_pool(name="ps", bufs=1))
+
+        picks = sb.tile([P, J // 16], U16, name="picks")
+        places = sb.tile([P, N // 16], U16, name="places")
+        xs = sb.tile([P, PASSES * T], U8, name="xs", align_bytes=64)
+        ws = sb.tile([P, PASSES * N], U8, name="ws", align_bytes=64)
+        xw = [sb.tile([P, T], U16, name="xw%d" % z, align_bytes=64) for z in range(PASSES)]
+        wa = sb.tile([P, PASSES * 2 * N], U8, name="wa", align_bytes=64)
+        wb_raw = [sb.tile([P, PACK, N], F32, name="wb_raw%d" % z, align_bytes=64) for z in range(PASSES)]
+        wb_bf = [sb.tile([P, N, PACK], BF16, name="wb_bf%d" % z, align_bytes=64) for z in range(PASSES)]
+        wb_codes = [sb.tile([P, N], U32, name="wb_codes%d" % z, align_bytes=64) for z in range(PASSES)]
+        wb_scales = [sb.tile([P, N], U8, name="wb_scales%d" % z, align_bytes=64) for z in range(PASSES)]
+        bi_col = sb.tile([P, N // P], F32, name="bi_col")
+        bias = sb.tile([P, N], F32, name="bias", align_bytes=64)
+        ident = sb.tile([P, P], F32, name="ident", align_bytes=64)
+        olds = [sb.tile([P, C], F32, name="old%d" % j, align_bytes=64) for j in range(TILES)]
+        pages = [sb.tile([P, C], F32, name="page%d" % j, align_bytes=64) for j in range(TILES)]
+        gs = sb.tile([P, PASSES * J], U8, name="gs", align_bytes=64)
+        gw = [[sb.tile([P, P], U16, name="gw%d_%d" % (j, z), align_bytes=64) for z in range(PASSES)] for j in range(TILES)]
+        a_ps = [ps.tile([P, N], F32, name="a_ps%d" % j) for j in range(TILES)]
+        b_ps = [ps.tile([P, N], F32, name="b_ps%d" % j) for j in range(TILES)]
+
+        nc.gpsimd.memset(xs[:].bitcast(I32), 0)
+        nc.vector.memset(ws[:].bitcast(I32), 0)
+        for j in range(TILES):
+            nc.vector.memset(pages[j][:], 0.0)
+        nc.gpsimd.dma_start(bi_col[:], bi.rearrange("o (p c) -> p (o c)", p=P))
+        make_identity(nc, ident[:])
+
+        def load_wb(z):
+            nc.sync.dma_start(wb_raw[z][:], wb[z * K_PASS : (z + 1) * K_PASS, :].rearrange("(p t) n -> p t n", t=PACK))
+
+        nc.sync.dma_start(picks[:], offs)
+        nc.sync.dma_start(xw[0][:].bitcast(I32), xt_words[0].bitcast(I32))
+        load_scale_rows(nc, xs, xt_scales)
+        load_wb(0)
+        load_wb(1)
+        load_scale_rows(nc, ws, wa_scales)
+        nc.sync.dma_start(
+            wa[:].bitcast(I32).rearrange("p (z c) -> p z c", z=PASSES),
+            wa_words.bitcast(I32).rearrange("z p c -> p z c"),
+        )
+        nc.sync.dma_start(xw[1][:].bitcast(I32), xt_words[1].bitcast(I32))
+        nc.sync.dma_start(places[:], offs2)
+        for j in range(TILES):
+            nc.sync.dma_start(olds[j][:], old[j * P : (j + 1) * P, :])
+
+        def gather_words(j, z):
+            nc.vector.tensor_copy(gw[j][z][:], xw[z][:].indirect(picks[:, j * LIST_COLS : (j + 1) * LIST_COLS]))
+
+        def quantise_wb(z):
+            dst, src = interleave_views(wb_bf[z], wb_raw[z], V_COLS[z], N)
+            nc.scalar.activation(dst, src, COPY)
+            dst, src = interleave_views(wb_bf[z], wb_raw[z], 0, V_COLS[z])
+            nc.vector.tensor_copy(dst, src)
+            nc.vector.quantize_mx(
+                out=wb_codes[z][:].bitcast(E5M2X4),
+                scales=wb_scales[z][:],
+                in_=wb_bf[z][:].rearrange("p n t -> p (n t)"),
+            )
+
+        def multiply(acc, j, z, codes, scales):
+            nc.tensor.matmul_mx(
+                out=acc[:],
+                lhsT=gw[j][z][:].bitcast(FP4X4),
+                lhsT_scale=gs[:, z * J + j * P : z * J + (j + 1) * P],
+                rhs=codes,
+                rhs_scale=scales,
+                start=(z == 0),
+                stop=(z == PASSES - 1),
+            )
+
+        def multiply_pass(j, z):
+            multiply(b_ps[j], j, z, wb_codes[z][:].bitcast(E5M2X4), wb_scales[z][:])
+            multiply(a_ps[j], j, z, wa[:, z * 2 * N : (z + 1) * 2 * N].bitcast(FP4X4), ws[:, z * N : (z + 1) * N])
+
+        for j in range(TILES):
+            gather_words(j, 0)
+        for z in range(PASSES):
+            nc.vector.tensor_copy(gs[:, z * J : (z + 1) * J], xs[:, z * T : (z + 1) * T].indirect(picks[:]))
+        for z in range(PASSES):
+            quantise_wb(z)
+
+        bias_ps = ps.tile([P, N // P, P], F32, name="bias_ps")
+        for c in range(N // P):
+            nc.tensor.transpose(bias_ps[:, c, :], bi_col[:, c : c + 1].to_broadcast([P, P]), ident[:])
+        nc.scalar.activation(
+            bias[:].rearrange("q (p c) -> q p c", c=N // P), bias_ps[:].rearrange("q c p -> q p c"), COPY
+        )
+
+        for j in range(TILES):
+            multiply_pass(j, 0)
+        for j in range(TILES):
+            gather_words(j, 1)
+            multiply_pass(j, 1)
+
+        b2 = [sb.tile([P, N], F32, name="b2_%d" % j, align_bytes=64) for j in range(TILES)]
+        ds = [sb.tile([P, N], F32, name="d%d" % j, align_bytes=64) for j in range(TILES)]
+        for j in range(TILES):
+            nc.vector.tensor_tensor(b2[j][:], b_ps[j][:], bias[:], ALU.add)
+            nc.vector.tensor_tensor(ds[j][:], a_ps[j][:], b2[j][:], ALU.max)
+
+        nc.scalar.activation(pages[0][:].indirect(places[:]), ds[0][:], COPY)
+        nc.vector.tensor_copy(pages[1][:].indirect(places[:, 0:LIST_COLS]), ds[1][:, 0:P])
+        nc.scalar.activation(pages[1][:].indirect(places[:, LIST_COLS : 2 * LIST_COLS]), ds[1][:, P : 2 * P], COPY)
+
+        for j in range(TILES):
+            for c0 in range(0, C, OUT_COLS):
+                cols = slice(c0, c0 + OUT_COLS)
+                res = sb.tile([P, OUT_COLS], F32, name="res%d_%d" % (j, c0), align_bytes=64)
+                nc.vector.scalar_tensor_tensor(res[:], olds[j][:, cols], -0.4, pages[j][:, cols], ALU.mult, ALU.add)
+                nc.sync.dma_start(out[j * P : (j + 1) * P, cols], res[:])

@@ -23,8 +23,10 @@ K_PASS = P * PACK
 PASSES = K // K_PASS
 TILES = J // P
 LIST_COLS = P // 16
-V_COLS = (64, 160)
-OUT_COLS = 512
+BANK = 2048
+D1_START = 448
+D1_STEP = 640
+OUT_CUTS = ((0, 512, 1024), (0, 512, 768, 1024))
 
 
 def interleave_views(grouped, raw, c0, c1):
@@ -34,10 +36,10 @@ def interleave_views(grouped, raw, c0, c1):
 
 
 def load_scale_rows(nc, plane, scales):
-    for q in range(4):
+    for r in range(4):
         nc.sync.dma_start(
-            plane[32 * q : 32 * q + 4, :].bitcast(I32).rearrange("r (z c) -> r z c", z=PASSES),
-            scales[:, 4 * q : 4 * q + 4, :].bitcast(I32).rearrange("z r c -> r z c"),
+            plane[r:P:32, :].bitcast(I32).rearrange("q (z c) -> q z c", z=PASSES),
+            scales[:, r:16:4, :].bitcast(I32).rearrange("z q c -> q z c"),
         )
 
 
@@ -60,20 +62,16 @@ def tile_list_rows_onetoken_placedrows_kernel(
         wb_codes = [sb.tile([P, N], U32, name="wb_codes%d" % z, align_bytes=64) for z in range(PASSES)]
         wb_scales = [sb.tile([P, N], U8, name="wb_scales%d" % z, align_bytes=64) for z in range(PASSES)]
         bi_col = sb.tile([P, N // P], F32, name="bi_col")
-        bias = sb.tile([P, N], F32, name="bias", align_bytes=64)
         ident = sb.tile([P, P], F32, name="ident", align_bytes=64)
         olds = [sb.tile([P, C], F32, name="old%d" % j, align_bytes=64) for j in range(TILES)]
         pages = [sb.tile([P, C], F32, name="page%d" % j, align_bytes=64) for j in range(TILES)]
         gs = sb.tile([P, PASSES * J], U8, name="gs", align_bytes=64)
-        gw = [[sb.tile([P, P], U16, name="gw%d_%d" % (j, z), align_bytes=64) for z in range(PASSES)] for j in range(TILES)]
-        a_ps = [ps.tile([P, N], F32, name="a_ps%d" % j) for j in range(TILES)]
-        b_ps = [ps.tile([P, N], F32, name="b_ps%d" % j) for j in range(TILES)]
+        gw = {}
 
         nc.gpsimd.memset(xs[:].bitcast(I32), 0)
         nc.vector.memset(ws[:].bitcast(I32), 0)
         for j in range(TILES):
             nc.vector.memset(pages[j][:], 0.0)
-        nc.gpsimd.dma_start(bi_col[:], bi.rearrange("o (p c) -> p (o c)", p=P))
         make_identity(nc, ident[:])
 
         def load_wb(z):
@@ -81,26 +79,26 @@ def tile_list_rows_onetoken_placedrows_kernel(
 
         nc.sync.dma_start(picks[:], offs)
         nc.sync.dma_start(xw[0][:].bitcast(I32), xt_words[0].bitcast(I32))
+        nc.sync.dma_start(bi_col[:], bi.rearrange("o (p c) -> p (o c)", p=P))
         load_scale_rows(nc, xs, xt_scales)
         load_wb(0)
         load_wb(1)
-        load_scale_rows(nc, ws, wa_scales)
         nc.sync.dma_start(
             wa[:].bitcast(I32).rearrange("p (z c) -> p z c", z=PASSES),
             wa_words.bitcast(I32).rearrange("z p c -> p z c"),
         )
+        load_scale_rows(nc, ws, wa_scales)
         nc.sync.dma_start(xw[1][:].bitcast(I32), xt_words[1].bitcast(I32))
         nc.sync.dma_start(places[:], offs2)
         for j in range(TILES):
             nc.sync.dma_start(olds[j][:], old[j * P : (j + 1) * P, :])
 
-        def gather_words(j, z):
-            nc.vector.tensor_copy(gw[j][z][:], xw[z][:].indirect(picks[:, j * LIST_COLS : (j + 1) * LIST_COLS]))
+        def gather_words(j, z, tag):
+            gw[j, z] = sb.tile([P, P], U16, name="gw%d_%d" % (j, z), tag=tag, align_bytes=64)
+            nc.vector.tensor_copy(gw[j, z][:], xw[z][:].indirect(picks[:, j * LIST_COLS : (j + 1) * LIST_COLS]))
 
         def quantise_wb(z):
-            dst, src = interleave_views(wb_bf[z], wb_raw[z], V_COLS[z], N)
-            nc.scalar.activation(dst, src, COPY)
-            dst, src = interleave_views(wb_bf[z], wb_raw[z], 0, V_COLS[z])
+            dst, src = interleave_views(wb_bf[z], wb_raw[z], 0, N)
             nc.vector.tensor_copy(dst, src)
             nc.vector.quantize_mx(
                 out=wb_codes[z][:].bitcast(E5M2X4),
@@ -111,7 +109,7 @@ def tile_list_rows_onetoken_placedrows_kernel(
         def multiply(acc, j, z, codes, scales):
             nc.tensor.matmul_mx(
                 out=acc[:],
-                lhsT=gw[j][z][:].bitcast(FP4X4),
+                lhsT=gw[j, z][:].bitcast(FP4X4),
                 lhsT_scale=gs[:, z * J + j * P : z * J + (j + 1) * P],
                 rhs=codes,
                 rhs_scale=scales,
@@ -119,43 +117,60 @@ def tile_list_rows_onetoken_placedrows_kernel(
                 stop=(z == PASSES - 1),
             )
 
-        def multiply_pass(j, z):
+        def multiply_b(j, z):
             multiply(b_ps[j], j, z, wb_codes[z][:].bitcast(E5M2X4), wb_scales[z][:])
+
+        def multiply_a(j, z):
             multiply(a_ps[j], j, z, wa[:, z * 2 * N : (z + 1) * 2 * N].bitcast(FP4X4), ws[:, z * N : (z + 1) * N])
 
         for j in range(TILES):
-            gather_words(j, 0)
+            gather_words(j, 0, "words%d" % j)
         for z in range(PASSES):
             nc.vector.tensor_copy(gs[:, z * J : (z + 1) * J], xs[:, z * T : (z + 1) * T].indirect(picks[:]))
         for z in range(PASSES):
             quantise_wb(z)
 
-        bias_ps = ps.tile([P, N // P, P], F32, name="bias_ps")
+        bias = sb.tile([P, N], F32, name="bias", align_bytes=64)
+        staging = ps.tile([P, 2 * TILES * BANK // 4], F32, name="staging", offset=0)
+        bias_ps = staging[:, 0:N].rearrange("q (c p) -> q c p", p=P)
         for c in range(N // P):
             nc.tensor.transpose(bias_ps[:, c, :], bi_col[:, c : c + 1].to_broadcast([P, P]), ident[:])
         nc.scalar.activation(
-            bias[:].rearrange("q (p c) -> q p c", c=N // P), bias_ps[:].rearrange("q c p -> q p c"), COPY
+            bias[:].rearrange("q (p c) -> q p c", c=N // P), bias_ps.rearrange("q c p -> q p c"), COPY
         )
 
+        b_ps = [ps.tile([P, N], F32, name="b_ps%d" % j, offset=2 * j * BANK) for j in range(TILES)]
+        a_ps = [ps.tile([P, N], F32, name="a_ps%d" % j, offset=(2 * j + 1) * BANK) for j in range(TILES)]
         for j in range(TILES):
-            multiply_pass(j, 0)
+            multiply_b(j, 0)
+        for j in reversed(range(TILES)):
+            multiply_a(j, 0)
         for j in range(TILES):
-            gather_words(j, 1)
-            multiply_pass(j, 1)
+            gather_words(j, 1, ("words2", "words1")[j])
+            multiply_b(j, 1)
+        for j in range(TILES):
+            multiply_a(j, 1)
 
+        d0 = sb.tile([P, N], F32, name="d0", align_bytes=64)
+        shared = sb.tile([P, D1_START + 2 * D1_STEP], F32, name="shared", align_bytes=64)
+        d1 = shared[:, D1_START:].rearrange("p (h x) -> p h x", h=2)[:, :, 0:P]
+        ds = [d0[:].rearrange("p (h x) -> p h x", h=2), d1]
         b2 = [sb.tile([P, N], F32, name="b2_%d" % j, align_bytes=64) for j in range(TILES)]
-        ds = [sb.tile([P, N], F32, name="d%d" % j, align_bytes=64) for j in range(TILES)]
         for j in range(TILES):
             nc.vector.tensor_tensor(b2[j][:], b_ps[j][:], bias[:], ALU.add)
-            nc.vector.tensor_tensor(ds[j][:], a_ps[j][:], b2[j][:], ALU.max)
-
-        nc.scalar.activation(pages[0][:].indirect(places[:]), ds[0][:], COPY)
-        nc.vector.tensor_copy(pages[1][:].indirect(places[:, 0:LIST_COLS]), ds[1][:, 0:P])
-        nc.scalar.activation(pages[1][:].indirect(places[:, LIST_COLS : 2 * LIST_COLS]), ds[1][:, P : 2 * P], COPY)
-
         for j in range(TILES):
-            for c0 in range(0, C, OUT_COLS):
-                cols = slice(c0, c0 + OUT_COLS)
-                res = sb.tile([P, OUT_COLS], F32, name="res%d_%d" % (j, c0), align_bytes=64)
-                nc.vector.scalar_tensor_tensor(res[:], olds[j][:, cols], -0.4, pages[j][:, cols], ALU.mult, ALU.add)
-                nc.sync.dma_start(out[j * P : (j + 1) * P, cols], res[:])
+            nc.vector.tensor_tensor(
+                ds[j], a_ps[j][:].rearrange("p (h x) -> p h x", h=2), b2[j][:].rearrange("p (h x) -> p h x", h=2), ALU.max
+            )
+
+        nc.scalar.activation(pages[0][:].indirect(places[:]), d0[:], COPY)
+        nc.vector.tensor_copy(pages[1][:].indirect(places[:, 0:LIST_COLS]), d1[:, 0, :])
+        nc.scalar.activation(pages[1][:].indirect(places[:, LIST_COLS : 2 * LIST_COLS]), d1[:, 1, :], COPY)
+
+        res1 = sb.tile([P, C], F32, name="res1", align_bytes=64)
+        res = [shared, res1]
+        for j in range(TILES):
+            for c0, c1 in zip(OUT_CUTS[j][:-1], OUT_CUTS[j][1:]):
+                cols = slice(c0, c1)
+                nc.vector.scalar_tensor_tensor(res[j][:, cols], olds[j][:, cols], -0.4, pages[j][:, cols], ALU.mult, ALU.add)
+                nc.sync.dma_start(out[j * P : (j + 1) * P, cols], res[j][:, cols])

from contextlib import ExitStack

import concourse.mybir as mybir
from concourse.masks import make_identity

K, T, J, N, C = 1024, 1024, 256, 256, 1024
FLOPS = 2 * 2 * K * J * N

F32 = mybir.dt.float32
BF16 = mybir.dt.bfloat16
I32 = mybir.dt.int32
U32 = mybir.dt.uint32
U16 = mybir.dt.uint16
U8 = mybir.dt.uint8
FP4X4 = mybir.dt.float4_e2m1fn_x4
E5M2X4 = mybir.dt.float8_e5m2_x4
ALU = mybir.AluOpType
COPY = mybir.ActivationFunctionType.Copy

P = 128
PACK = 4
K_PASS = P * PACK
PASSES = K // K_PASS
TILES = J // P
LIST_COLS = P // 16
BANK = 2048
D1_START = 448
D1_STEP = 640
OUT_CUTS = ((0, 512, 1024), (0, 512, 768, 1024))


def interleave_views(grouped, raw, c0, c1):
    dst = grouped[:, c0:c1, :].rearrange("p (c i) t -> p c t i", i=4)
    src = raw[:, :, c0:c1].rearrange("p t (c i) -> p c t i", i=4)
    return dst, src


def load_scale_rows(nc, plane, scales):
    for r in range(4):
        nc.sync.dma_start(
            plane[r:P:32, :].bitcast(I32).rearrange("q (z c) -> q z c", z=PASSES),
            scales[:, r:16:4, :].bitcast(I32).rearrange("z q c -> q z c"),
        )


def tile_list_rows_onetoken_placedrows_kernel(
    tc, xt_words, xt_scales, wa_words, wa_scales, wb, bi, old, offs, offs2, out
):
    nc = tc.nc
    with ExitStack() as ctx:
        sb = ctx.enter_context(tc.tile_pool(name="sb", bufs=1))
        ps = ctx.enter_context(tc.psum_pool(name="ps", bufs=1))

        picks = sb.tile([P, J // 16], U16, name="picks")
        places = sb.tile([P, N // 16], U16, name="places")
        xs = sb.tile([P, PASSES * T], U8, name="xs", align_bytes=64)
        ws = sb.tile([P, PASSES * N], U8, name="ws", align_bytes=64)
        xw = [sb.tile([P, T], U16, name="xw%d" % z, align_bytes=64) for z in range(PASSES)]
        wa = sb.tile([P, PASSES * 2 * N], U8, name="wa", align_bytes=64)
        wb_raw = [sb.tile([P, PACK, N], F32, name="wb_raw%d" % z, align_bytes=64) for z in range(PASSES)]
        wb_bf = [sb.tile([P, N, PACK], BF16, name="wb_bf%d" % z, align_bytes=64) for z in range(PASSES)]
        wb_codes = [sb.tile([P, N], U32, name="wb_codes%d" % z, align_bytes=64) for z in range(PASSES)]
        wb_scales = [sb.tile([P, N], U8, name="wb_scales%d" % z, align_bytes=64) for z in range(PASSES)]
        bi_col = sb.tile([P, N // P], F32, name="bi_col")
        ident = sb.tile([P, P], F32, name="ident", align_bytes=64)
        olds = [sb.tile([P, C], F32, name="old%d" % j, align_bytes=64) for j in range(TILES)]
        pages = [sb.tile([P, C], F32, name="page%d" % j, align_bytes=64) for j in range(TILES)]
        gs = sb.tile([P, PASSES * J], U8, name="gs", align_bytes=64)
        gw = {}

        nc.gpsimd.memset(xs[:].bitcast(I32), 0)
        nc.vector.memset(ws[:].bitcast(I32), 0)
        for j in range(TILES):
            nc.vector.memset(pages[j][:], 0.0)
        make_identity(nc, ident[:])

        def load_wb(z):
            nc.sync.dma_start(wb_raw[z][:], wb[z * K_PASS : (z + 1) * K_PASS, :].rearrange("(p t) n -> p t n", t=PACK))

        nc.sync.dma_start(picks[:], offs)
        nc.sync.dma_start(xw[0][:].bitcast(I32), xt_words[0].bitcast(I32))
        nc.sync.dma_start(bi_col[:], bi.rearrange("o (p c) -> p (o c)", p=P))
        load_scale_rows(nc, xs, xt_scales)
        load_wb(0)
        load_wb(1)
        nc.sync.dma_start(
            wa[:].bitcast(I32).rearrange("p (z c) -> p z c", z=PASSES),
            wa_words.bitcast(I32).rearrange("z p c -> p z c"),
        )
        load_scale_rows(nc, ws, wa_scales)
        nc.sync.dma_start(xw[1][:].bitcast(I32), xt_words[1].bitcast(I32))
        nc.sync.dma_start(places[:], offs2)
        for j in range(TILES):
            nc.sync.dma_start(olds[j][:], old[j * P : (j + 1) * P, :])

        def gather_words(j, z, tag):
            gw[j, z] = sb.tile([P, P], U16, name="gw%d_%d" % (j, z), tag=tag, align_bytes=64)
            nc.vector.tensor_copy(gw[j, z][:], xw[z][:].indirect(picks[:, j * LIST_COLS : (j + 1) * LIST_COLS]))

        def quantise_wb(z):
            dst, src = interleave_views(wb_bf[z], wb_raw[z], 0, N)
            nc.vector.tensor_copy(dst, src)
            nc.vector.quantize_mx(
                out=wb_codes[z][:].bitcast(E5M2X4),
                scales=wb_scales[z][:],
                in_=wb_bf[z][:].rearrange("p n t -> p (n t)"),
            )

        def multiply(acc, j, z, codes, scales):
            nc.tensor.matmul_mx(
                out=acc[:],
                lhsT=gw[j, z][:].bitcast(FP4X4),
                lhsT_scale=gs[:, z * J + j * P : z * J + (j + 1) * P],
                rhs=codes,
                rhs_scale=scales,
                start=(z == 0),
                stop=(z == PASSES - 1),
            )

        def multiply_b(j, z):
            multiply(b_ps[j], j, z, wb_codes[z][:].bitcast(E5M2X4), wb_scales[z][:])

        def multiply_a(j, z):
            multiply(a_ps[j], j, z, wa[:, z * 2 * N : (z + 1) * 2 * N].bitcast(FP4X4), ws[:, z * N : (z + 1) * N])

        for j in range(TILES):
            gather_words(j, 0, "words%d" % j)
        for z in range(PASSES):
            nc.vector.tensor_copy(gs[:, z * J : (z + 1) * J], xs[:, z * T : (z + 1) * T].indirect(picks[:]))
        for z in range(PASSES):
            quantise_wb(z)

        bias = sb.tile([P, N], F32, name="bias", align_bytes=64)
        staging = ps.tile([P, 2 * TILES * BANK // 4], F32, name="staging", offset=0)
        bias_ps = staging[:, 0:N].rearrange("q (c p) -> q c p", p=P)
        for c in range(N // P):
            nc.tensor.transpose(bias_ps[:, c, :], bi_col[:, c : c + 1].to_broadcast([P, P]), ident[:])
        nc.scalar.activation(
            bias[:].rearrange("q (p c) -> q p c", c=N // P), bias_ps.rearrange("q c p -> q p c"), COPY
        )

        b_ps = [ps.tile([P, N], F32, name="b_ps%d" % j, offset=2 * j * BANK) for j in range(TILES)]
        a_ps = [ps.tile([P, N], F32, name="a_ps%d" % j, offset=(2 * j + 1) * BANK) for j in range(TILES)]
        for j in range(TILES):
            multiply_b(j, 0)
        for j in reversed(range(TILES)):
            multiply_a(j, 0)
        for j in range(TILES):
            gather_words(j, 1, ("words2", "words1")[j])
            multiply_b(j, 1)
        for j in range(TILES):
            multiply_a(j, 1)

        d0 = sb.tile([P, N], F32, name="d0", align_bytes=64)
        shared = sb.tile([P, D1_START + 2 * D1_STEP], F32, name="shared", align_bytes=64)
        d1 = shared[:, D1_START:].rearrange("p (h x) -> p h x", h=2)[:, :, 0:P]
        ds = [d0[:].rearrange("p (h x) -> p h x", h=2), d1]
        b2 = [sb.tile([P, N], F32, name="b2_%d" % j, align_bytes=64) for j in range(TILES)]
        for j in range(TILES):
            nc.vector.tensor_tensor(b2[j][:], b_ps[j][:], bias[:], ALU.add)
        for j in range(TILES):
            nc.vector.tensor_tensor(
                ds[j], a_ps[j][:].rearrange("p (h x) -> p h x", h=2), b2[j][:].rearrange("p (h x) -> p h x", h=2), ALU.max
            )

        nc.scalar.activation(pages[0][:].indirect(places[:]), d0[:], COPY)
        nc.vector.tensor_copy(pages[1][:].indirect(places[:, 0:LIST_COLS]), d1[:, 0, :])
        nc.scalar.activation(pages[1][:].indirect(places[:, LIST_COLS : 2 * LIST_COLS]), d1[:, 1, :], COPY)

        res1 = sb.tile([P, C], F32, name="res1", align_bytes=64)
        res = [shared, res1]
        for j in range(TILES):
            for c0, c1 in zip(OUT_CUTS[j][:-1], OUT_CUTS[j][1:]):
                cols = slice(c0, c1)
                nc.vector.scalar_tensor_tensor(res[j][:, cols], olds[j][:, cols], -0.4, pages[j][:, cols], ALU.mult, ALU.add)
                nc.sync.dma_start(out[j * P : (j + 1) * P, cols], res[j][:, cols])
